import numpy as np, ml_dtypes
CORES = [10,18,34,42,58,66,82,90,98,106]
N = 10
KT, FB, TK = 1, 128, 128
def setup_inputs(rng):
    return {"x": rng.standard_normal((N, 128, KT * TK), dtype=np.float32).astype(ml_dtypes.bfloat16), "w": rng.standard_normal((N, 128, KT * N * FB), dtype=np.float32).astype(ml_dtypes.bfloat16)}
def setup_inputs_big(rng):
    d = setup_inputs(rng)
    for k in ("x", "w"): d[k] = (d[k].astype(np.float32) * 1024.0).astype(d[k].dtype)
    return d
def setup_inputs_small(rng):
    d = setup_inputs(rng)
    for k in ("x", "w"): d[k] = (d[k].astype(np.float32) * (1 / 1024.0)).astype(d[k].dtype)
    return d
def setup_inputs_apart(rng):
    d = setup_inputs(rng)
    f = (10.0 ** rng.permutation(np.linspace(-1.5, 1.5, N))).astype(np.float32).reshape(N, 1, 1)
    for k in ("x", "w"): d[k] = (d[k].astype(np.float32) * f).astype(d[k].dtype)
    return d
def reference(x, w):
    X, W = x.astype(np.float64), w.astype(np.float64)
    y = np.zeros((N, FB, N * TK))
    for j in range(N):
        for r in range(N):
            for t in range(KT):
                y[r][:, TK * j:TK * j + TK] += W[j][:, FB * (N * t + r):FB * (N * t + r) + FB].T @ X[j][:, TK * t:TK * t + TK]
    return {"y": y.astype(ml_dtypes.bfloat16 if x.dtype != np.float64 else np.float64)}

@@ -1,0 +1,163 @@
+from concourse.bass import DstId, RemoteDMATransfer
+
+N = 10
+B = 128
+PLAN = [("direct", [[1]]),
+        ("direct", [[2], [3], [4], [5]]),
+        ("direct", [[6], [7], [8], [9]])]
+LATE = [6, 7, 8, 9]
+NC = len(PLAN)
+RELAY = max([len(p) for kind, parts in PLAN for p in parts])
+
+SCRATCH = {
+    "xs": ("sbuf", [128, B], "bfloat16"),
+    "ws": ("sbuf", [128, N * B], "bfloat16"),
+    "snd": ("sbuf", [128, (N - 1) * B], "bfloat16"),
+    "land": ("sbuf", [128, N * B], "bfloat16"),
+    "relay": ("sbuf", [128, RELAY * B], "bfloat16"),
+    "psown": ("psum", [128, 512], "float32"),
+}
+SEMAPHORES = ["mmown", "own", "sent", "hin", "arrE", "arrL", "stS", "stC"]
+for _k in range(NC):
+    SCRATCH["ps%d" % _k] = ("psum", [128, 512], "float32")
+    SEMAPHORES += ["ld%d" % _k, "mm%d" % _k, "cp%d" % _k]
+
+
+def _runs(blocks):
+    out = []
+    for b in sorted(blocks):
+        if out and out[-1][1] == b:
+            out[-1][1] = b + 1
+        else:
+            out.append([b, b + 1])
+    return sorted(out, key=lambda r: r[0] - r[1])
+
+
+def _cols(lo, hi):
+    return slice(lo * B, hi * B)
+
+
+def _split(mask, k):
+    bits = [1 << b for b in range(mask.bit_length()) if (mask >> b) & 1]
+    per = len(bits) // k
+    return [sum(bits[i * per:(i + 1) * per]) for i in range(k)], per
+
+
+def _away(core, T, topo):
+    m = -1
+    for d in T.cores:
+        if topo.chip(d) != topo.chip(core):
+            m &= topo.mask(core, d)
+    return m
+
+
+def _helpers(c, T, topo):
+    hs = [h for h in range(topo.CORES_PER_CHIP * topo.CHIPS)
+          if h != c and topo.chip(h) == topo.chip(c) and all(topo.may_write(h, d) for d in T.cores)]
+    return sorted(hs, key=lambda h: (topo.die(h) == topo.die(c), h))
+
+
+def _transfer(topo, d, mask, sem, src, dst):
+    rid, pid = topo.addr(d)[0:2]
+    return RemoteDMATransfer(dst_ids=[DstId(rid=rid, pnc=pid)], dma_engine_mask=mask, remote_sem=sem, src=src, dst=dst)
+
+
+def _helper_program(g, core, T, topo):
+    S = T.sem
+    for c in T.cores:
+        if topo.chip(c) != topo.chip(core):
+            continue
+        j = T.rank_of(c)
+        hs = _helpers(c, T, topo)
+        for kind, parts in PLAN:
+            if kind != "push" or core not in hs[0:len(parts)]:
+                continue
+            part = parts[hs.index(core)]
+            g.wait_ge(S.hin, _split(topo.mask(c, core) & ~_away(c, T, topo), len(parts))[1])
+            masks, per = _split(_away(core, T, topo), len(part))
+            g.remote_dma_fused([_transfer(topo, T.cores[(j + s) % N], masks[i], S.arrL if s in LATE else S.arrE,
+                                          T.relay[:, _cols(i, i + 1)], T.land[:, _cols(j, j + 1)])
+                                for i, s in enumerate(part)], local_sem=S.sent)
+            g.wait_ge(S.sent, per * len(part))
+
+
+def rank_program(g, core, T, topo):
+    j = T.rank_of(core)
+    if j is None:
+        _helper_program(g, core, T, topo)
+        return
+    S = T.sem
+    queues = [g.sync, g.scalar]
+    steps = [[s for p in parts for s in p] for kind, parts in PLAN]
+
+    need = [[(j + s) % N for s in st] for st in steps]
+    need[-1] = need[-1] + [j]
+    g.sync.dma_start(T.xs[:], T.x[:]).then_inc(S.ld0, 16)
+    ld_total = [16] + [0] * (NC - 1)
+    turn = 1
+    for k in range(NC):
+        for lo, hi in _runs(need[k]):
+            queues[turn % 2].dma_start(T.ws[:, _cols(lo, hi)], T.w[:, _cols(lo, hi)]).then_inc(S["ld%d" % k], 16)
+            ld_total[k] += 16
+            turn += 1
+
+    for k in range(NC):
+        g.tensor.wait_ge(S["ld%d" % k], ld_total[k])
+        for i, s in enumerate(steps[k]):
+            r = (j + s) % N
+            g.tensor.matmul(T["ps%d" % k][:, _cols(i, i + 1)], T.ws[:, _cols(r, r + 1)], T.xs[:],
+                            start=True, stop=True).then_inc(S["mm%d" % k], 1)
+    g.tensor.matmul(T.psown[:, 0:B], T.ws[:, _cols(j, j + 1)], T.xs[:], start=True, stop=True).then_inc(S.mmown, 1)
+    first = [sum(len(st) for st in steps[0:k]) for k in range(NC)]
+    for k in range(NC):
+        n = len(steps[k])
+        g.vector.wait_ge(S["mm%d" % k], n)
+        g.vector.tensor_copy(T.snd[:, _cols(first[k], first[k] + n)], T["ps%d" % k][:, 0:n * B]).then_inc(S["cp%d" % k], 1)
+    g.vector.wait_ge(S.mmown, 1)
+    g.vector.tensor_copy(T.land[:, _cols(j, j + 1)], T.psown[:, 0:B]).then_inc(S.own, 1)
+
+    away = _away(core, T, topo)
+    hs = _helpers(core, T, topo)
+    sent = 0
+    inc = {}
+    for k, (kind, parts) in enumerate(PLAN):
+        g.wait_ge(S["cp%d" % k], 1)
+        trs = []
+        pos = first[k]
+        if kind == "direct":
+            masks, per = _split(away, len(parts))
+            for i, (s,) in enumerate(parts):
+                trs.append(_transfer(topo, T.cores[(j + s) % N], masks[i], S.arrL if s in LATE else S.arrE,
+                                     T.snd[:, _cols(pos + i, pos + i + 1)], T.land[:, _cols(j, j + 1)]))
+                inc[s] = per
+        else:
+            masks, per = _split(topo.mask(core, hs[0]) & ~away, len(parts))
+            for i, p in enumerate(parts):
+                trs.append(_transfer(topo, hs[i], masks[i], S.hin,
+                                     T.snd[:, _cols(pos, pos + len(p))], T.relay[:, _cols(0, len(p))]))
+                pos += len(p)
+                for s in p:
+                    inc[s] = _split(_away(hs[i], T, topo), len(p))[1]
+        sent += per * len(parts)
+        g.remote_dma_fused(trs, local_sem=S.sent)
+
+    e_runs = _runs([j] + [(j - s) % N for s in inc if s not in LATE])
+    l_runs = _runs([(j - s) % N for s in LATE])
+    n_early = sum(inc[s] for s in inc if s not in LATE)
+    n_late = sum(inc[s] for s in LATE)
+    st = [S.stS, S.stC]
+    st_total = [0, 0]
+    for q, (lo, hi) in enumerate(e_runs):
+        queues[q].wait_ge(S.arrE, n_early)
+        queues[q].wait_ge(S.own, 1)
+        queues[q].dma_start(T.y[:, _cols(lo, hi)], T.land[:, _cols(lo, hi)]).then_inc(st[q], 16)
+        st_total[q] += 16
+    for i, (lo, hi) in enumerate(l_runs):
+        q = (i + 1) % 2
+        queues[q].wait_ge(S.arrL, n_late)
+        queues[q].dma_start(T.y[:, _cols(lo, hi)], T.land[:, _cols(lo, hi)]).then_inc(st[q], 16)
+        st_total[q] += 16
+    for q in range(2):
+        if st_total[q]:
+            queues[q].wait_ge(st[q], st_total[q])
+    g.wait_ge(S.sent, sent)

@@ -2,25 +2,25 @@ from concourse.bass import DstId, RemoteDMATransfer
 
 N = 10
 B = 128
-PLAN = [("direct", [[1]]),
-        ("direct", [[2], [3], [4], [5]]),
-        ("direct", [[6], [7], [8], [9]])]
-LATE = [6, 7, 8, 9]
-NC = len(PLAN)
-RELAY = max([len(p) for kind, parts in PLAN for p in parts])
+SIZES = [2, 4, 2]
+NC = len(SIZES)
+SLOTS = 2
 
 SCRATCH = {
     "xs": ("sbuf", [128, B], "bfloat16"),
     "ws": ("sbuf", [128, N * B], "bfloat16"),
-    "snd": ("sbuf", [128, (N - 1) * B], "bfloat16"),
+    "snd": ("sbuf", [128, (N - 2) * B], "bfloat16"),
     "land": ("sbuf", [128, N * B], "bfloat16"),
-    "relay": ("sbuf", [128, RELAY * B], "bfloat16"),
+    "raw": ("sbuf", [128, SLOTS * 2 * B], "bfloat16"),
     "psown": ("psum", [128, 512], "float32"),
 }
-SEMAPHORES = ["mmown", "own", "sent", "hin", "arrE", "arrL", "stS", "stC"]
+SEMAPHORES = ["ldq", "mmown", "own", "sent", "arrE", "arrL", "stS", "stC"]
 for _k in range(NC):
     SCRATCH["ps%d" % _k] = ("psum", [128, 512], "float32")
     SEMAPHORES += ["ld%d" % _k, "mm%d" % _k, "cp%d" % _k]
+for _k in range(SLOTS):
+    SCRATCH["psr%d" % _k] = ("psum", [128, 512], "float32")
+    SEMAPHORES += ["rin%d" % _k, "mmr%d" % _k]
 
 
 def _runs(blocks):
@@ -51,10 +51,32 @@ def _away(core, T, topo):
     return m
 
 
-def _helpers(c, T, topo):
-    hs = [h for h in range(topo.CORES_PER_CHIP * topo.CHIPS)
-          if h != c and topo.chip(h) == topo.chip(c) and all(topo.may_write(h, d) for d in T.cores)]
-    return sorted(hs, key=lambda h: (topo.die(h) == topo.die(c), h))
+def _first_dest(T, topo):
+    chips = [topo.chip(c) for c in T.cores]
+    mate = [[r for r in range(N) if topo.mates(chips[j], chips[r])] for j in range(N)]
+    q = [m[0] if m else None for m in mate]
+    taken = []
+    for j in range(N):
+        if q[j] is None:
+            q[j] = [r for r in range(N) if topo.same_plane(chips[j], chips[r]) and mate[r] and r not in taken][0]
+            taken.append(q[j])
+    return q
+
+
+def _plans(T, topo):
+    q = _first_dest(T, topo)
+    used = [(q[j] - j) % N for j in range(N)]
+    n = SIZES[-1]
+    late = [list(range(s, s + n)) for s in range(1, N - n + 1) if not [t for t in range(s, s + n) if t in used]][-1]
+    calls = []
+    for j in range(N):
+        rest = [s for s in range(1, N) if s not in late and s != used[j]]
+        cs = []
+        for m in SIZES[0:-1]:
+            cs.append(rest[0:m])
+            rest = rest[m:]
+        calls.append(cs + [late])
+    return q, late, calls
 
 
 def _transfer(topo, d, mask, sem, src, dst):
@@ -62,45 +84,30 @@ def _transfer(topo, d, mask, sem, src, dst):
     return RemoteDMATransfer(dst_ids=[DstId(rid=rid, pnc=pid)], dma_engine_mask=mask, remote_sem=sem, src=src, dst=dst)
 
 
-def _helper_program(g, core, T, topo):
-    S = T.sem
-    for c in T.cores:
-        if topo.chip(c) != topo.chip(core):
-            continue
-        j = T.rank_of(c)
-        hs = _helpers(c, T, topo)
-        for kind, parts in PLAN:
-            if kind != "push" or core not in hs[0:len(parts)]:
-                continue
-            part = parts[hs.index(core)]
-            g.wait_ge(S.hin, _split(topo.mask(c, core) & ~_away(c, T, topo), len(parts))[1])
-            masks, per = _split(_away(core, T, topo), len(part))
-            g.remote_dma_fused([_transfer(topo, T.cores[(j + s) % N], masks[i], S.arrL if s in LATE else S.arrE,
-                                          T.relay[:, _cols(i, i + 1)], T.land[:, _cols(j, j + 1)])
-                                for i, s in enumerate(part)], local_sem=S.sent)
-            g.wait_ge(S.sent, per * len(part))
-
-
 def rank_program(g, core, T, topo):
     j = T.rank_of(core)
     if j is None:
-        _helper_program(g, core, T, topo)
         return
     S = T.sem
     queues = [g.sync, g.scalar]
-    steps = [[s for p in parts for s in p] for kind, parts in PLAN]
+    q, late, calls = _plans(T, topo)
+    steps = calls[j]
+    away = _away(core, T, topo)
+    givers = [i for i in range(N) if q[i] == j]
 
-    need = [[(j + s) % N for s in st] for st in steps]
+    g.sync.dma_start(T.xs[:], T.x[:]).then_inc(S.ldq, 16)
+    g.scalar.dma_start(T.ws[:, _cols(q[j], q[j] + 1)], T.w[:, _cols(q[j], q[j] + 1)]).then_inc(S.ldq, 16)
+    need = [[(j + s) % N for s in st_] for st_ in steps]
     need[-1] = need[-1] + [j]
-    g.sync.dma_start(T.xs[:], T.x[:]).then_inc(S.ld0, 16)
-    ld_total = [16] + [0] * (NC - 1)
-    turn = 1
+    ld_total = [0] * NC
+    turn = 0
     for k in range(NC):
         for lo, hi in _runs(need[k]):
             queues[turn % 2].dma_start(T.ws[:, _cols(lo, hi)], T.w[:, _cols(lo, hi)]).then_inc(S["ld%d" % k], 16)
             ld_total[k] += 16
             turn += 1
 
+    g.tensor.wait_ge(S.ldq, 32)
     for k in range(NC):
         g.tensor.wait_ge(S["ld%d" % k], ld_total[k])
         for i, s in enumerate(steps[k]):
@@ -108,56 +115,64 @@ def rank_program(g, core, T, topo):
             g.tensor.matmul(T["ps%d" % k][:, _cols(i, i + 1)], T.ws[:, _cols(r, r + 1)], T.xs[:],
                             start=True, stop=True).then_inc(S["mm%d" % k], 1)
     g.tensor.matmul(T.psown[:, 0:B], T.ws[:, _cols(j, j + 1)], T.xs[:], start=True, stop=True).then_inc(S.mmown, 1)
-    first = [sum(len(st) for st in steps[0:k]) for k in range(NC)]
+    first = [sum(SIZES[0:k]) for k in range(NC)]
     for k in range(NC):
-        n = len(steps[k])
+        n = SIZES[k]
         g.vector.wait_ge(S["mm%d" % k], n)
         g.vector.tensor_copy(T.snd[:, _cols(first[k], first[k] + n)], T["ps%d" % k][:, 0:n * B]).then_inc(S["cp%d" % k], 1)
     g.vector.wait_ge(S.mmown, 1)
     g.vector.tensor_copy(T.land[:, _cols(j, j + 1)], T.psown[:, 0:B]).then_inc(S.own, 1)
 
-    away = _away(core, T, topo)
-    hs = _helpers(core, T, topo)
-    sent = 0
-    inc = {}
-    for k, (kind, parts) in enumerate(PLAN):
-        g.wait_ge(S["cp%d" % k], 1)
-        trs = []
-        pos = first[k]
-        if kind == "direct":
-            masks, per = _split(away, len(parts))
-            for i, (s,) in enumerate(parts):
-                trs.append(_transfer(topo, T.cores[(j + s) % N], masks[i], S.arrL if s in LATE else S.arrE,
-                                     T.snd[:, _cols(pos + i, pos + i + 1)], T.land[:, _cols(j, j + 1)]))
-                inc[s] = per
-        else:
-            masks, per = _split(topo.mask(core, hs[0]) & ~away, len(parts))
-            for i, p in enumerate(parts):
-                trs.append(_transfer(topo, hs[i], masks[i], S.hin,
-                                     T.snd[:, _cols(pos, pos + len(p))], T.relay[:, _cols(0, len(p))]))
-                pos += len(p)
-                for s in p:
-                    inc[s] = _split(_away(hs[i], T, topo), len(p))[1]
-        sent += per * len(parts)
-        g.remote_dma_fused(trs, local_sem=S.sent)
+    masks2, per2 = _split(away, 2)
+    for k, i in enumerate(givers):
+        g.tensor.wait_ge(S["rin%d" % k], 2 * _split(_away(T.cores[i], T, topo), 2)[1])
+        g.tensor.matmul(T["psr%d" % k][:, 0:B], T.raw[:, _cols(2 * k + 1, 2 * k + 2)], T.raw[:, _cols(2 * k, 2 * k + 1)],
+                        start=True, stop=True).then_inc(S["mmr%d" % k], 1)
+        g.vector.wait_ge(S["mmr%d" % k], 1)
+        g.vector.tensor_copy(T.land[:, _cols(i, i + 1)], T["psr%d" % k][:, 0:B]).then_inc(S.own, 1)
 
-    e_runs = _runs([j] + [(j - s) % N for s in inc if s not in LATE])
-    l_runs = _runs([(j - s) % N for s in LATE])
-    n_early = sum(inc[s] for s in inc if s not in LATE)
-    n_late = sum(inc[s] for s in LATE)
+    slot = [i for i in range(N) if q[i] == q[j]].index(j)
+    d = T.cores[q[j]]
+    g.wait_ge(S.ldq, 32)
+    g.remote_dma_fused([_transfer(topo, d, masks2[0], S["rin%d" % slot], T.xs[:], T.raw[:, _cols(2 * slot, 2 * slot + 1)]),
+                        _transfer(topo, d, masks2[1], S["rin%d" % slot], T.ws[:, _cols(q[j], q[j] + 1)],
+                                  T.raw[:, _cols(2 * slot + 1, 2 * slot + 2)])], local_sem=S.sent)
+    sent = 2 * per2
+    for k, st_ in enumerate(steps):
+        g.wait_ge(S["cp%d" % k], 1)
+        masks, per = _split(away, len(st_))
+        g.remote_dma_fused([_transfer(topo, T.cores[(j + s) % N], masks[i], S.arrL if k == NC - 1 else S.arrE,
+                                      T.snd[:, _cols(first[k] + i, first[k] + i + 1)], T.land[:, _cols(j, j + 1)])
+                            for i, s in enumerate(st_)], local_sem=S.sent)
+        sent += per * len(st_)
+
+    n_early = 0
+    n_late = 0
+    for i in range(N):
+        for k, st_ in enumerate(calls[i]):
+            if (j - i) % N in st_:
+                per = _split(_away(T.cores[i], T, topo), len(st_))[1]
+                if k == NC - 1:
+                    n_late += per
+                else:
+                    n_early += per
+
+    l_blocks = [(j - s) % N for s in late]
+    e_runs = _runs([b for b in range(N) if b not in l_blocks])
+    l_runs = _runs(l_blocks)
     st = [S.stS, S.stC]
     st_total = [0, 0]
-    for q, (lo, hi) in enumerate(e_runs):
-        queues[q].wait_ge(S.arrE, n_early)
-        queues[q].wait_ge(S.own, 1)
-        queues[q].dma_start(T.y[:, _cols(lo, hi)], T.land[:, _cols(lo, hi)]).then_inc(st[q], 16)
-        st_total[q] += 16
+    for p, (lo, hi) in enumerate(e_runs):
+        queues[p].wait_ge(S.arrE, n_early)
+        queues[p].wait_ge(S.own, 1 + len(givers))
+        queues[p].dma_start(T.y[:, _cols(lo, hi)], T.land[:, _cols(lo, hi)]).then_inc(st[p], 16)
+        st_total[p] += 16
     for i, (lo, hi) in enumerate(l_runs):
-        q = (i + 1) % 2
-        queues[q].wait_ge(S.arrL, n_late)
-        queues[q].dma_start(T.y[:, _cols(lo, hi)], T.land[:, _cols(lo, hi)]).then_inc(st[q], 16)
-        st_total[q] += 16
-    for q in range(2):
-        if st_total[q]:
-            queues[q].wait_ge(st[q], st_total[q])
+        p = (i + 1) % 2
+        queues[p].wait_ge(S.arrL, n_late)
+        queues[p].dma_start(T.y[:, _cols(lo, hi)], T.land[:, _cols(lo, hi)]).then_inc(st[p], 16)
+        st_total[p] += 16
+    for p in range(2):
+        if st_total[p]:
+            queues[p].wait_ge(st[p], st_total[p])
     g.wait_ge(S.sent, sent)

from concourse.bass import DstId, RemoteDMATransfer

N = 10
B = 128
SIZES = [2, 4, 2]
NC = len(SIZES)
SLOTS = 2

SCRATCH = {
    "xs": ("sbuf", [128, B], "bfloat16"),
    "ws": ("sbuf", [128, N * B], "bfloat16"),
    "snd": ("sbuf", [128, (N - 2) * B], "bfloat16"),
    "land": ("sbuf", [128, N * B], "bfloat16"),
    "raw": ("sbuf", [128, SLOTS * 2 * B], "bfloat16"),
    "psown": ("psum", [128, 512], "float32"),
}
SEMAPHORES = ["ldq", "mmown", "own", "sent", "arrE", "arrL", "stS", "stC"]
for _k in range(NC):
    SCRATCH["ps%d" % _k] = ("psum", [128, 512], "float32")
    SEMAPHORES += ["ld%d" % _k, "mm%d" % _k, "cp%d" % _k]
for _k in range(SLOTS):
    SCRATCH["psr%d" % _k] = ("psum", [128, 512], "float32")
    SEMAPHORES += ["rin%d" % _k, "mmr%d" % _k]


def _runs(blocks):
    out = []
    for b in sorted(blocks):
        if out and out[-1][1] == b:
            out[-1][1] = b + 1
        else:
            out.append([b, b + 1])
    return sorted(out, key=lambda r: r[0] - r[1])


def _cols(lo, hi):
    return slice(lo * B, hi * B)


def _split(mask, k):
    bits = [1 << b for b in range(mask.bit_length()) if (mask >> b) & 1]
    per = len(bits) // k
    return [sum(bits[i * per:(i + 1) * per]) for i in range(k)], per


def _away(core, T, topo):
    m = -1
    for d in T.cores:
        if topo.chip(d) != topo.chip(core):
            m &= topo.mask(core, d)
    return m


def _first_dest(T, topo):
    chips = [topo.chip(c) for c in T.cores]
    mate = [[r for r in range(N) if topo.mates(chips[j], chips[r])] for j in range(N)]
    q = [m[0] if m else None for m in mate]
    taken = []
    for j in range(N):
        if q[j] is None:
            q[j] = [r for r in range(N) if topo.same_plane(chips[j], chips[r]) and mate[r] and r not in taken][0]
            taken.append(q[j])
    return q


def _plans(T, topo):
    q = _first_dest(T, topo)
    used = [(q[j] - j) % N for j in range(N)]
    n = SIZES[-1]
    late = [list(range(s, s + n)) for s in range(1, N - n + 1) if not [t for t in range(s, s + n) if t in used]][-1]
    calls = []
    for j in range(N):
        rest = [s for s in range(1, N) if s not in late and s != used[j]]
        cs = []
        for m in SIZES[0:-1]:
            cs.append(rest[0:m])
            rest = rest[m:]
        calls.append(cs + [late])
    return q, late, calls


def _transfer(topo, d, mask, sem, src, dst):
    rid, pid = topo.addr(d)[0:2]
    return RemoteDMATransfer(dst_ids=[DstId(rid=rid, pnc=pid)], dma_engine_mask=mask, remote_sem=sem, src=src, dst=dst)


def rank_program(g, core, T, topo):
    j = T.rank_of(core)
    if j is None:
        return
    S = T.sem
    queues = [g.sync, g.scalar]
    q, late, calls = _plans(T, topo)
    steps = calls[j]
    away = _away(core, T, topo)
    givers = [i for i in range(N) if q[i] == j]

    g.sync.dma_start(T.xs[:], T.x[:]).then_inc(S.ldq, 16)
    g.scalar.dma_start(T.ws[:, _cols(q[j], q[j] + 1)], T.w[:, _cols(q[j], q[j] + 1)]).then_inc(S.ldq, 16)
    need = [[(j + s) % N for s in st_] for st_ in steps]
    need[-1] = need[-1] + [j]
    ld_total = [0] * NC
    turn = 0
    for k in range(NC):
        for lo, hi in _runs(need[k]):
            queues[turn % 2].dma_start(T.ws[:, _cols(lo, hi)], T.w[:, _cols(lo, hi)]).then_inc(S["ld%d" % k], 16)
            ld_total[k] += 16
            turn += 1

    g.tensor.wait_ge(S.ldq, 32)
    for k in range(NC):
        g.tensor.wait_ge(S["ld%d" % k], ld_total[k])
        for i, s in enumerate(steps[k]):
            r = (j + s) % N
            g.tensor.matmul(T["ps%d" % k][:, _cols(i, i + 1)], T.ws[:, _cols(r, r + 1)], T.xs[:],
                            start=True, stop=True).then_inc(S["mm%d" % k], 1)
    g.tensor.matmul(T.psown[:, 0:B], T.ws[:, _cols(j, j + 1)], T.xs[:], start=True, stop=True).then_inc(S.mmown, 1)
    first = [sum(SIZES[0:k]) for k in range(NC)]
    for k in range(NC):
        n = SIZES[k]
        g.vector.wait_ge(S["mm%d" % k], n)
        g.vector.tensor_copy(T.snd[:, _cols(first[k], first[k] + n)], T["ps%d" % k][:, 0:n * B]).then_inc(S["cp%d" % k], 1)
    g.vector.wait_ge(S.mmown, 1)
    g.vector.tensor_copy(T.land[:, _cols(j, j + 1)], T.psown[:, 0:B]).then_inc(S.own, 1)

    masks2, per2 = _split(away, 2)
    for k, i in enumerate(givers):
        g.tensor.wait_ge(S["rin%d" % k], 2 * _split(_away(T.cores[i], T, topo), 2)[1])
        g.tensor.matmul(T["psr%d" % k][:, 0:B], T.raw[:, _cols(2 * k + 1, 2 * k + 2)], T.raw[:, _cols(2 * k, 2 * k + 1)],
                        start=True, stop=True).then_inc(S["mmr%d" % k], 1)
        g.vector.wait_ge(S["mmr%d" % k], 1)
        g.vector.tensor_copy(T.land[:, _cols(i, i + 1)], T["psr%d" % k][:, 0:B]).then_inc(S.own, 1)

    slot = [i for i in range(N) if q[i] == q[j]].index(j)
    d = T.cores[q[j]]
    g.wait_ge(S.ldq, 32)
    g.remote_dma_fused([_transfer(topo, d, masks2[0], S["rin%d" % slot], T.xs[:], T.raw[:, _cols(2 * slot, 2 * slot + 1)]),
                        _transfer(topo, d, masks2[1], S["rin%d" % slot], T.ws[:, _cols(q[j], q[j] + 1)],
                                  T.raw[:, _cols(2 * slot + 1, 2 * slot + 2)])], local_sem=S.sent)
    sent = 2 * per2
    for k, st_ in enumerate(steps):
        g.wait_ge(S["cp%d" % k], 1)
        masks, per = _split(away, len(st_))
        g.remote_dma_fused([_transfer(topo, T.cores[(j + s) % N], masks[i], S.arrL if k == NC - 1 else S.arrE,
                                      T.snd[:, _cols(first[k] + i, first[k] + i + 1)], T.land[:, _cols(j, j + 1)])
                            for i, s in enumerate(st_)], local_sem=S.sent)
        sent += per * len(st_)

    n_early = 0
    n_late = 0
    for i in range(N):
        for k, st_ in enumerate(calls[i]):
            if (j - i) % N in st_:
                per = _split(_away(T.cores[i], T, topo), len(st_))[1]
                if k == NC - 1:
                    n_late += per
                else:
                    n_early += per

    l_blocks = [(j - s) % N for s in late]
    e_runs = _runs([b for b in range(N) if b not in l_blocks])
    l_runs = _runs(l_blocks)
    st = [S.stS, S.stC]
    st_total = [0, 0]
    for p, (lo, hi) in enumerate(e_runs):
        queues[p].wait_ge(S.arrE, n_early)
        queues[p].wait_ge(S.own, 1 + len(givers))
        queues[p].dma_start(T.y[:, _cols(lo, hi)], T.land[:, _cols(lo, hi)]).then_inc(st[p], 16)
        st_total[p] += 16
    for i, (lo, hi) in enumerate(l_runs):
        p = (i + 1) % 2
        queues[p].wait_ge(S.arrL, n_late)
        queues[p].dma_start(T.y[:, _cols(lo, hi)], T.land[:, _cols(lo, hi)]).then_inc(st[p], 16)
        st_total[p] += 16
    for p in range(2):
        if st_total[p]:
            queues[p].wait_ge(st[p], st_total[p])
    g.wait_ge(S.sent, sent)
